import numpy as np
import ml_dtypes


def mxq(x, axis, fmt="e4m3"):
    dtype, down = {"e4m3": (ml_dtypes.float8_e4m3fn, 7), "e5m2": (ml_dtypes.float8_e5m2, 14)}[fmt]
    v = np.moveaxis(np.asarray(x, np.float32).astype(ml_dtypes.bfloat16).astype(np.float64), axis, -1)
    blocks = v.reshape(v.shape[:-1] + (-1, 32))
    amax = np.abs(blocks).max(-1, keepdims=True)
    byte = np.maximum(np.where(amax > 0, np.frexp(amax)[1] - 1 + 127, 0) - down, 1)
    scale = np.exp2(byte - 127.0)
    codes = (blocks / scale).astype(np.float32).astype(dtype).astype(np.float64)
    return np.moveaxis((codes * scale).reshape(v.shape), -1, axis)


WIDE = False


def mx_kscale(k):
    if not WIDE:
        return np.ones(k)
    levels = np.array([10, -10, 5, -5, 0])
    if k % 512:
        return np.exp2(np.random.permutation(np.resize(levels, k // 32))).repeat(32)
    a = np.empty((k // 512, 16))
    for p in range(k // 512):
        a[p, :8] = np.random.permutation(np.resize(levels, 8))
        for g in range(8):
            far = levels[np.abs(levels - a[p, g]) >= 10]
            a[p, g + 8] = far[np.random.randint(len(far))]
    return np.exp2(a.ravel()).repeat(32)


def f64(x):
    return np.asarray(x).astype(np.float64)


def striped(idx):
    return np.tile(idx.reshape(-1, 16).T, (8, 1)).astype(np.uint16)


def unstriped(offs):
    return offs[:16].T.reshape(-1).astype(np.int64)


def striped8(idx):
    return np.concatenate([x.reshape(-1, 16).T for x in idx]).astype(np.uint16)


def runs(offs, k):
    lists = np.stack([offs[16 * r : 16 * r + 16].T.reshape(-1) for r in range(8)]).astype(np.int64)
    return lists[np.arange(k) % 512 // 64]


def pack_weight(w):
    k, n = w.shape
    w = f64(np.asarray(w, np.float32).astype(ml_dtypes.bfloat16)).reshape(k // 32, 32, n)
    amax = np.abs(w).max(1)
    byte = np.clip(np.where(amax > 0, np.frexp(amax)[1] - 1 + 127 - 7, 1), 1, 254)
    scaled = (w * np.exp2(127.0 - byte)[:, None, :]).reshape(k, n).astype(np.float32)
    words = np.ascontiguousarray(scaled.reshape(k // 512, 128, 4, n).transpose(0, 1, 3, 2)).astype(ml_dtypes.float8_e4m3fn).view(np.uint8)
    return words, np.ascontiguousarray(byte.astype(np.uint8).reshape(k // 512, 16, n))


def unpack_weight(words, scales):
    g, p, n, _ = words.shape
    vals = np.ascontiguousarray(words).view(ml_dtypes.float8_e4m3fn).astype(np.float64) * np.repeat(np.exp2(scales.astype(np.float64) - 127.0), 8, axis=1)[..., None]
    return vals.transpose(0, 1, 3, 2).reshape(g * 512, n)


K, T, S, V, N, H = 512, 2048, 1024, 512, 512, 512


def setup_inputs():
    n = np.random.standard_normal
    s = mx_kscale(K)[:, None]
    u = mx_kscale(H)
    packed_xT = pack_weight(n((K, T)) * s)
    return {
        "x_words": packed_xT[0],
        "x_scales": packed_xT[1],
        "w1": (n((K, H)) / np.sqrt(K) / s).astype(np.float32),
        "gn": (np.random.uniform(0.5, 1.5, (H, 1)) * u[:, None]).astype(np.float32),
        "w2": (n((H, N)) / np.sqrt(H) / u[:, None]).astype(np.float32),
        "offs": striped(np.random.permutation(T)[:S]),
        "order": striped8(np.stack([np.random.permutation(S) for _ in range(8)])),
        "n1": striped8(np.stack([np.random.permutation(V) for _ in range(8)])),
        "n2": striped8(np.stack([np.random.permutation(V) for _ in range(8)])),
    }


def reference(x_words, x_scales, w1, gn, w2, offs, order, n1, n2):
    xq = unpack_weight(x_words, x_scales)[:, unstriped(offs)]
    y = mxq(f64(w1), 0, "e4m3").T @ xq
    o = y[np.arange(H)[:, None], runs(order, H)]
    mx = o.reshape(H, V, 2).max(axis=2)
    mn = o.reshape(H, V, 2).min(axis=2)
    z = f64(gn) * (mx * np.tanh(mn))
    h = mxq(f64(w2), 0, "e4m3").T @ mxq(z, 0, "e4m3")
    return h - (0.5 * (h[np.arange(N)[:, None], runs(n1, N)] + h[np.arange(N)[:, None], runs(n2, N)]))

@@ -1,0 +1,201 @@
+from contextlib import ExitStack
+
+import concourse.mybir as mybir
+
+K, T, S, V, N, H = 512, 2048, 1024, 512, 512, 512
+FLOPS = 2 * K * H * S + 2 * H * N * V
+
+F32 = mybir.dt.float32
+BF16 = mybir.dt.bfloat16
+I32 = mybir.dt.int32
+U32 = mybir.dt.uint32
+U16 = mybir.dt.uint16
+U8 = mybir.dt.uint8
+FP8X4 = mybir.dt.float8_e4m3fn_x4
+ALU = mybir.AluOpType
+ACT = mybir.ActivationFunctionType
+
+P = 128
+PACK = 4
+LANES = 16
+BANK = 512
+HALVES = 2
+VH = V // HALVES
+TINY = 1e-30
+W1_VECTOR_M = 40
+
+
+def deal_views(grouped, raw, m0, m1):
+    dst = grouped[:].rearrange("p t m j -> p m j t")[:, m0:m1]
+    src = raw[:].rearrange("p j (m t) -> p m j t", t=PACK)[:, m0:m1]
+    return dst, src
+
+
+def tile_picked_prodpool_none_p_kernel(
+    tc, x_words, x_scales, w1, gn, w2, offs, order, n1, n2, out
+):
+    nc = tc.nc
+    with ExitStack() as ctx:
+        keep = ctx.enter_context(tc.tile_pool(name="keep", bufs=1))
+        ring = ctx.enter_context(tc.tile_pool(name="ring", bufs=3))
+        psum = ctx.enter_context(tc.psum_pool(name="psum", bufs=1))
+
+        offs_sb = keep.tile([P, S // LANES], U16, name="offs_sb")
+        order_sb = keep.tile([P, S // LANES], U16, name="order_sb")
+        n1_sb = keep.tile([P, V // LANES], U16, name="n1_sb")
+        n2_sb = keep.tile([P, V // LANES], U16, name="n2_sb")
+        all_words = keep.tile([P, T], U32, name="all_words", align_bytes=64)
+        all_scales = keep.tile([P, T], U8, name="all_scales", align_bytes=64)
+        w1_raw = keep.tile([P, PACK, H], F32, name="w1_raw", align_bytes=64)
+        w2_raw = keep.tile([P, PACK, N], F32, name="w2_raw", align_bytes=64)
+        gain = keep.tile([P, PACK], F32, name="gain")
+
+        nc.vector.memset(all_scales[:].bitcast(I32), 0)
+        nc.sync.dma_start(offs_sb[:], offs)
+        for q in range(4):
+            nc.scalar.dma_start(
+                out=all_scales[32 * q : 32 * q + 4, :].bitcast(I32),
+                in_=x_scales[0, 4 * q : 4 * q + 4, :].bitcast(I32),
+            )
+        nc.sync.dma_start(out=w1_raw[:], in_=w1.rearrange("(p j) c -> p j c", j=PACK))
+        nc.sync.dma_start(
+            out=all_words[:].bitcast(I32),
+            in_=x_words[0].rearrange("p n r -> p (n r)").bitcast(I32),
+        )
+        nc.scalar.dma_start(out=gain[:], in_=gn.rearrange("(p t) o -> p (t o)", t=PACK))
+        nc.sync.dma_start(order_sb[:], order)
+        nc.sync.dma_start(out=w2_raw[:], in_=w2.rearrange("(p j) c -> p j c", j=PACK))
+        nc.sync.dma_start(n1_sb[:], n1)
+        nc.sync.dma_start(n2_sb[:], n2)
+
+        x_planes = keep.tile([P, S], U8, name="x_planes", align_bytes=64)
+        x_codes = keep.tile([P, S], U32, name="x_codes", align_bytes=64)
+        nc.vector.tensor_copy(x_planes[:], all_scales[:].indirect(offs_sb[:]))
+
+        gain_abs = keep.tile([P, PACK], F32, name="gain_abs")
+        gain_safe = keep.tile([P, PACK], F32, name="gain_safe")
+        gain_inv = keep.tile([P, PACK], F32, name="gain_inv")
+        nc.scalar.activation(gain_abs[:], gain[:], ACT.Abs)
+        nc.vector.scalar_tensor_tensor(gain_safe[:], gain_abs[:], TINY, gain[:], ALU.is_lt, ALU.add)
+        nc.vector.reciprocal(gain_inv[:], gain_safe[:])
+
+        w1_grouped = keep.tile([P, PACK, P, PACK], BF16, name="w1_grouped", align_bytes=64)
+        w1_codes = keep.tile([P, H], U32, name="w1_codes", align_bytes=64)
+        w1_planes = keep.tile([P, H], U8, name="w1_planes", align_bytes=64)
+        dst, src = deal_views(w1_grouped, w1_raw, 0, W1_VECTOR_M)
+        nc.vector.tensor_copy(dst, src)
+        dst, src = deal_views(w1_grouped, w1_raw, W1_VECTOR_M, P)
+        nc.scalar.copy(dst, src)
+
+        nc.vector.quantize_mx(
+            out=w1_codes[:].bitcast(FP8X4),
+            scales=w1_planes[:],
+            in_=w1_grouped[:].rearrange("p t m j -> p (t m j)"),
+        )
+        y = [keep.tile([P, S], F32, name="y%d" % t) for t in range(PACK)]
+        banks = {}
+        for c in range(S // BANK):
+            picked = slice(c * BANK, (c + 1) * BANK)
+            nc.vector.tensor_copy(
+                x_codes[:, picked], all_words[:].indirect(offs_sb[:, c * BANK // LANES : (c + 1) * BANK // LANES])
+            )
+            for t in range(PACK):
+                cols = slice(t * P, (t + 1) * P)
+                banks[t, c] = psum.tile([P, BANK], F32, name="bank%d" % (2 * t + c))
+                nc.tensor.matmul_mx(
+                    out=banks[t, c][:],
+                    lhsT=w1_codes[:, cols].bitcast(FP8X4),
+                    lhsT_scale=w1_planes[:, cols],
+                    rhs=x_codes[:, picked].bitcast(FP8X4),
+                    rhs_scale=x_planes[:, picked],
+                    start=True,
+                    stop=True,
+                )
+        for t in range(PACK):
+            for c in range(S // BANK):
+                picked = slice(c * BANK, (c + 1) * BANK)
+                if t == 0 and c == 1:
+                    nc.vector.tensor_scalar(y[t][:, picked], banks[t, c][:], gain_abs[:, t : t + 1], None, ALU.mult)
+                else:
+                    nc.scalar.activation(y[t][:, picked], banks[t, c][:], ACT.Copy, scale=gain_abs[:, t : t + 1])
+
+        w2_grouped = keep.tile([P, PACK, P, PACK], BF16, name="w2_grouped", align_bytes=64)
+        w2_codes = keep.tile([P, N], U32, name="w2_codes", align_bytes=64)
+        w2_planes = keep.tile([P, N], U8, name="w2_planes", align_bytes=64)
+
+        h_plain = [keep.tile([P, V], F32, name="h_plain%d" % t) for t in range(PACK)]
+        h_neg_half = [keep.tile([P, V], F32, name="h_neg_half%d" % t) for t in range(PACK)]
+
+        larger = [keep.tile([P, PACK, VH], F32, name="larger%d" % u) for u in range(HALVES)]
+        bent = [keep.tile([P, PACK, VH], F32, name="bent%d" % u) for u in range(HALVES)]
+        for t in range(PACK):
+            lined = [ring.tile([P, 2 * VH], F32, name="lined%d" % u) for u in range(HALVES)]
+            smaller = [ring.tile([P, VH], F32, name="smaller%d" % u) for u in range(HALVES)]
+            for u in range(HALVES):
+                entries = slice(u * 2 * VH // LANES, (u + 1) * 2 * VH // LANES)
+                nc.vector.tensor_copy(lined[u][:], y[t][:].indirect(order_sb[:, entries]))
+            for u in range(HALVES):
+                nc.vector.tensor_tensor(smaller[u][:], lined[u][:, 0::2], lined[u][:, 1::2], ALU.min)
+                nc.scalar.activation(bent[u][:, t, :], smaller[u][:], ACT.Tanh, scale=gain_inv[:, t : t + 1])
+            for u in range(HALVES):
+                nc.vector.tensor_tensor(larger[u][:, t, :], lined[u][:, 0::2], lined[u][:, 1::2], ALU.max)
+        dst, src = deal_views(w2_grouped, w2_raw, 0, P)
+        nc.scalar.copy(dst, src)
+        nc.vector.quantize_mx(
+            out=w2_codes[:].bitcast(FP8X4),
+            scales=w2_planes[:],
+            in_=w2_grouped[:].rearrange("p t m j -> p (t m j)"),
+        )
+        zs = []
+        for u in range(HALVES):
+            z = keep.tile([P, VH, PACK], BF16, name="z%d" % u, align_bytes=64)
+            nc.vector.tensor_tensor(
+                z[:].rearrange("p (c i) t -> p c t i", i=2),
+                larger[u][:].rearrange("p t (c i) -> p c t i", i=2),
+                bent[u][:].rearrange("p t (c i) -> p c t i", i=2),
+                ALU.mult,
+            )
+            zs.append(z)
+        for u in range(HALVES):
+            z = zs[u]
+            z_codes = keep.tile([P, VH], U32, name="z_codes%d" % u, align_bytes=64)
+            z_planes = keep.tile([P, VH], U8, name="z_planes%d" % u, align_bytes=64)
+            nc.vector.quantize_mx(
+                out=z_codes[:].bitcast(FP8X4), scales=z_planes[:], in_=z[:].rearrange("p v t -> p (v t)")
+            )
+            places = slice(u * VH, (u + 1) * VH)
+            for t in range(PACK):
+                cols = slice(t * P, (t + 1) * P)
+                bank = psum.tile([P, VH], F32, name="bank%d" % (2 * t + u))
+                nc.tensor.matmul_mx(
+                    out=bank[:],
+                    lhsT=w2_codes[:, cols].bitcast(FP8X4),
+                    lhsT_scale=w2_planes[:, cols],
+                    rhs=z_codes[:].bitcast(FP8X4),
+                    rhs_scale=z_planes[:],
+                    start=True,
+                    stop=True,
+                )
+                nc.scalar.activation(h_neg_half[t][:, places], bank[:], ACT.Copy, scale=-0.5)
+                nc.scalar.copy(h_plain[t][:, places], bank[:])
+
+        out_rows = out.rearrange("(p t) v -> p t v", t=PACK)
+        for t in range(PACK):
+            partial = ring.tile([P, V], F32, name="partial")
+            result = keep.tile([P, V], F32, name="result%d" % t)
+            for u in range(HALVES):
+                places = slice(u * VH, (u + 1) * VH)
+                entries = slice(u * VH // LANES, (u + 1) * VH // LANES)
+                nc.vector.tensor_tensor(
+                    partial[:, places], h_neg_half[t][:].indirect(n1_sb[:, entries]), h_plain[t][:, places], ALU.add
+                )
+            for u in range(HALVES):
+                places = slice(u * VH, (u + 1) * VH)
+                entries = slice(u * VH // LANES, (u + 1) * VH // LANES)
+                nc.vector.tensor_tensor(
+                    result[:, places], h_neg_half[t][:].indirect(n2_sb[:, entries]), partial[:, places], ALU.add
+                )
+                if t == PACK - 1:
+                    nc.sync.dma_start(out=out_rows[:, t, places], in_=result[:, places])
+            if t < PACK - 1:
+                nc.sync.dma_start(out=out_rows[:, t, :], in_=result[:])

@@ -25,10 +25,26 @@ TINY = 1e-30
 W1_VECTOR_M = 40
 
 
-def deal_views(grouped, raw, m0, m1):
-    dst = grouped[:].rearrange("p t m j -> p m j t")[:, m0:m1]
-    src = raw[:].rearrange("p j (m t) -> p m j t", t=PACK)[:, m0:m1]
+def deal_views(grouped, raw, tiles, cols):
+    dst = grouped[:].rearrange("p t m j -> p m j t")[:, cols]
+    src = raw[:].rearrange("p j (m t) -> p m j t", t=PACK)[:, cols, :, tiles]
     return dst, src
+
+
+def quantize(nc, codes, planes, values):
+    nc.vector.quantize_mx(out=codes.bitcast(FP8X4), scales=planes, in_=values)
+
+
+def product(nc, bank, w_codes, w_planes, codes, planes):
+    nc.tensor.matmul_mx(
+        out=bank,
+        lhsT=w_codes.bitcast(FP8X4),
+        lhsT_scale=w_planes,
+        rhs=codes.bitcast(FP8X4),
+        rhs_scale=planes,
+        start=True,
+        stop=True,
+    )
 
 
 def tile_picked_prodpool_none_p_kernel(
@@ -50,18 +66,17 @@ def tile_picked_prodpool_none_p_kernel(
         w2_raw = keep.tile([P, PACK, N], F32, name="w2_raw", align_bytes=64)
         gain = keep.tile([P, PACK], F32, name="gain")
 
-        nc.vector.memset(all_scales[:].bitcast(I32), 0)
         nc.sync.dma_start(offs_sb[:], offs)
         for q in range(4):
-            nc.scalar.dma_start(
-                out=all_scales[32 * q : 32 * q + 4, :].bitcast(I32),
-                in_=x_scales[0, 4 * q : 4 * q + 4, :].bitcast(I32),
+            nc.sync.dma_start(
+                out=all_scales[32 * q : 32 * q + 32, :].bitcast(I32),
+                in_=x_scales[0, 4 * q : 4 * q + 4, :].bitcast(I32).unsqueeze(0).broadcast_to([8, 4, T // 4]),
             )
-        nc.sync.dma_start(out=w1_raw[:], in_=w1.rearrange("(p j) c -> p j c", j=PACK))
         nc.sync.dma_start(
             out=all_words[:].bitcast(I32),
             in_=x_words[0].rearrange("p n r -> p (n r)").bitcast(I32),
         )
+        nc.sync.dma_start(out=w1_raw[:], in_=w1.rearrange("(p j) c -> p j c", j=PACK))
         nc.scalar.dma_start(out=gain[:], in_=gn.rearrange("(p t) o -> p (t o)", t=PACK))
         nc.sync.dma_start(order_sb[:], order)
         nc.sync.dma_start(out=w2_raw[:], in_=w2.rearrange("(p j) c -> p j c", j=PACK))
@@ -71,6 +86,7 @@ def tile_picked_prodpool_none_p_kernel(
         x_planes = keep.tile([P, S], U8, name="x_planes", align_bytes=64)
         x_codes = keep.tile([P, S], U32, name="x_codes", align_bytes=64)
         nc.vector.tensor_copy(x_planes[:], all_scales[:].indirect(offs_sb[:]))
+        nc.vector.tensor_copy(x_codes[:], all_words[:].indirect(offs_sb[:]))
 
         gain_abs = keep.tile([P, PACK], F32, name="gain_abs")
         gain_safe = keep.tile([P, PACK], F32, name="gain_safe")
@@ -79,105 +95,107 @@ def tile_picked_prodpool_none_p_kernel(
         nc.vector.scalar_tensor_tensor(gain_safe[:], gain_abs[:], TINY, gain[:], ALU.is_lt, ALU.add)
         nc.vector.reciprocal(gain_inv[:], gain_safe[:])
 
-        w1_grouped = keep.tile([P, PACK, P, PACK], BF16, name="w1_grouped", align_bytes=64)
+        w1_first = keep.tile([P, 1, P, PACK], BF16, name="w1_first", align_bytes=64)
+        w1_rest = keep.tile([P, PACK - 1, P, PACK], BF16, name="w1_rest", align_bytes=64)
         w1_codes = keep.tile([P, H], U32, name="w1_codes", align_bytes=64)
         w1_planes = keep.tile([P, H], U8, name="w1_planes", align_bytes=64)
-        dst, src = deal_views(w1_grouped, w1_raw, 0, W1_VECTOR_M)
+        dst, src = deal_views(w1_first, w1_raw, slice(0, 1), slice(0, P))
         nc.vector.tensor_copy(dst, src)
-        dst, src = deal_views(w1_grouped, w1_raw, W1_VECTOR_M, P)
+        dst, src = deal_views(w1_rest, w1_raw, slice(1, PACK), slice(0, P))
         nc.scalar.copy(dst, src)
 
-        nc.vector.quantize_mx(
-            out=w1_codes[:].bitcast(FP8X4),
-            scales=w1_planes[:],
-            in_=w1_grouped[:].rearrange("p t m j -> p (t m j)"),
-        )
         y = [keep.tile([P, S], F32, name="y%d" % t) for t in range(PACK)]
-        banks = {}
-        for c in range(S // BANK):
-            picked = slice(c * BANK, (c + 1) * BANK)
-            nc.vector.tensor_copy(
-                x_codes[:, picked], all_words[:].indirect(offs_sb[:, c * BANK // LANES : (c + 1) * BANK // LANES])
-            )
-            for t in range(PACK):
-                cols = slice(t * P, (t + 1) * P)
-                banks[t, c] = psum.tile([P, BANK], F32, name="bank%d" % (2 * t + c))
-                nc.tensor.matmul_mx(
-                    out=banks[t, c][:],
-                    lhsT=w1_codes[:, cols].bitcast(FP8X4),
-                    lhsT_scale=w1_planes[:, cols],
-                    rhs=x_codes[:, picked].bitcast(FP8X4),
-                    rhs_scale=x_planes[:, picked],
-                    start=True,
-                    stop=True,
-                )
         for t in range(PACK):
-            for c in range(S // BANK):
-                picked = slice(c * BANK, (c + 1) * BANK)
-                if t == 0 and c == 1:
-                    nc.vector.tensor_scalar(y[t][:, picked], banks[t, c][:], gain_abs[:, t : t + 1], None, ALU.mult)
+            cols = slice(t * P, (t + 1) * P)
+            grouped = w1_first[:, 0] if t == 0 else w1_rest[:, t - 1]
+            quantize(nc, w1_codes[:, cols], w1_planes[:, cols], grouped.rearrange("p m j -> p (m j)"))
+            width = BANK // 2 if t == 0 else BANK
+            for c in range(S // width):
+                picked = slice(c * width, (c + 1) * width)
+                bank = psum.tile([P, width], F32, name="bank%d" % (c if t == 0 else (2 * t + c + 2) % 8))
+                product(nc, bank[:], w1_codes[:, cols], w1_planes[:, cols], x_codes[:, picked], x_planes[:, picked])
+                if t == 0 and c % 2 == 1:
+                    nc.vector.tensor_scalar(y[t][:, picked], bank[:], gain_abs[:, t : t + 1], None, ALU.mult)
                 else:
-                    nc.scalar.activation(y[t][:, picked], banks[t, c][:], ACT.Copy, scale=gain_abs[:, t : t + 1])
+                    nc.scalar.activation(y[t][:, picked], bank[:], ACT.Copy, scale=gain_abs[:, t : t + 1])
 
         w2_grouped = keep.tile([P, PACK, P, PACK], BF16, name="w2_grouped", align_bytes=64)
         w2_codes = keep.tile([P, N], U32, name="w2_codes", align_bytes=64)
         w2_planes = keep.tile([P, N], U8, name="w2_planes", align_bytes=64)
-
         h_plain = [keep.tile([P, V], F32, name="h_plain%d" % t) for t in range(PACK)]
         h_neg_half = [keep.tile([P, V], F32, name="h_neg_half%d" % t) for t in range(PACK)]
-
         larger = [keep.tile([P, PACK, VH], F32, name="larger%d" % u) for u in range(HALVES)]
         bent = [keep.tile([P, PACK, VH], F32, name="bent%d" % u) for u in range(HALVES)]
-        for t in range(PACK):
-            lined = [ring.tile([P, 2 * VH], F32, name="lined%d" % u) for u in range(HALVES)]
-            smaller = [ring.tile([P, VH], F32, name="smaller%d" % u) for u in range(HALVES)]
-            for u in range(HALVES):
-                entries = slice(u * 2 * VH // LANES, (u + 1) * 2 * VH // LANES)
-                nc.vector.tensor_copy(lined[u][:], y[t][:].indirect(order_sb[:, entries]))
-            for u in range(HALVES):
-                nc.vector.tensor_tensor(smaller[u][:], lined[u][:, 0::2], lined[u][:, 1::2], ALU.min)
-                nc.scalar.activation(bent[u][:, t, :], smaller[u][:], ACT.Tanh, scale=gain_inv[:, t : t + 1])
-            for u in range(HALVES):
-                nc.vector.tensor_tensor(larger[u][:, t, :], lined[u][:, 0::2], lined[u][:, 1::2], ALU.max)
-        dst, src = deal_views(w2_grouped, w2_raw, 0, P)
-        nc.scalar.copy(dst, src)
-        nc.vector.quantize_mx(
-            out=w2_codes[:].bitcast(FP8X4),
-            scales=w2_planes[:],
-            in_=w2_grouped[:].rearrange("p t m j -> p (t m j)"),
-        )
-        zs = []
-        for u in range(HALVES):
-            z = keep.tile([P, VH, PACK], BF16, name="z%d" % u, align_bytes=64)
+        z = keep.tile([P, V, PACK], BF16, name="z", align_bytes=64)
+        z_codes = keep.tile([P, V], U32, name="z_codes", align_bytes=64)
+        z_planes = keep.tile([P, V], U8, name="z_planes", align_bytes=64)
+        lined = {}
+
+        def line_up(t, u):
+            lined[t, u] = keep.tile([P, 2 * VH], F32, name="lined%d_%d" % (t, u))
+            entries = slice(u * 2 * VH // LANES, (u + 1) * 2 * VH // LANES)
+            nc.vector.tensor_copy(lined[t, u][:], y[t][:].indirect(order_sb[:, entries]))
+
+        def pool_pairs(jobs):
+            for t, u in jobs:
+                smaller = keep.tile([P, VH], F32, name="smaller%d_%d" % (t, u))
+                nc.vector.tensor_tensor(smaller[:], lined[t, u][:, 0::2], lined[t, u][:, 1::2], ALU.min)
+                nc.scalar.activation(bent[u][:, t, :], smaller[:], ACT.Tanh, scale=gain_inv[:, t : t + 1])
+            for t, u in jobs:
+                nc.vector.tensor_tensor(larger[u][:, t, :], lined[t, u][:, 0::2], lined[t, u][:, 1::2], ALU.max)
+
+        def make_z(v0, v1):
+            u = v0 // VH
+            inside = slice(v0 - u * VH, v1 - u * VH)
             nc.vector.tensor_tensor(
-                z[:].rearrange("p (c i) t -> p c t i", i=2),
-                larger[u][:].rearrange("p t (c i) -> p c t i", i=2),
-                bent[u][:].rearrange("p t (c i) -> p c t i", i=2),
+                z[:, v0:v1, :].rearrange("p (c i) t -> p c t i", i=2),
+                larger[u][:, :, inside].rearrange("p t (c i) -> p c t i", i=2),
+                bent[u][:, :, inside].rearrange("p t (c i) -> p c t i", i=2),
                 ALU.mult,
             )
-            zs.append(z)
-        for u in range(HALVES):
-            z = zs[u]
-            z_codes = keep.tile([P, VH], U32, name="z_codes%d" % u, align_bytes=64)
-            z_planes = keep.tile([P, VH], U8, name="z_planes%d" % u, align_bytes=64)
-            nc.vector.quantize_mx(
-                out=z_codes[:].bitcast(FP8X4), scales=z_planes[:], in_=z[:].rearrange("p v t -> p (v t)")
-            )
-            places = slice(u * VH, (u + 1) * VH)
-            for t in range(PACK):
-                cols = slice(t * P, (t + 1) * P)
-                bank = psum.tile([P, VH], F32, name="bank%d" % (2 * t + u))
-                nc.tensor.matmul_mx(
-                    out=bank[:],
-                    lhsT=w2_codes[:, cols].bitcast(FP8X4),
-                    lhsT_scale=w2_planes[:, cols],
-                    rhs=z_codes[:].bitcast(FP8X4),
-                    rhs_scale=z_planes[:],
-                    start=True,
-                    stop=True,
-                )
-                nc.scalar.activation(h_neg_half[t][:, places], bank[:], ACT.Copy, scale=-0.5)
-                nc.scalar.copy(h_plain[t][:, places], bank[:])
+
+        def quantize_z(v0, v1):
+            quantize(nc, z_codes[:, v0:v1], z_planes[:, v0:v1], z[:, v0:v1, :].rearrange("p v t -> p (v t)"))
+
+        def make_h(t, v0, v1, slot):
+            cols = slice(t * P, (t + 1) * P)
+            bank = psum.tile([P, v1 - v0], F32, name="bank%d" % (2 * t + slot))
+            product(nc, bank[:], w2_codes[:, cols], w2_planes[:, cols], z_codes[:, v0:v1], z_planes[:, v0:v1])
+            return bank
+
+        def copy_out(t, v0, v1, bank):
+            nc.scalar.activation(h_neg_half[t][:, v0:v1], bank[:], ACT.Copy, scale=-0.5)
+            nc.scalar.copy(h_plain[t][:, v0:v1], bank[:])
+
+        for t in range(2):
+            for u in range(HALVES):
+                line_up(t, u)
+            pool_pairs([(t, u) for u in range(HALVES)])
+        for m0 in range(0, P, P // 2):
+            dst, src = deal_views(w2_grouped, w2_raw, slice(0, PACK), slice(m0, m0 + P // 2))
+            nc.scalar.copy(dst, src)
+        for t in range(2, PACK):
+            line_up(t, 0)
+        pool_pairs([(t, 0) for t in range(2, PACK)])
+        line_up(2, 1)
+        make_z(0, VH)
+        quantize(nc, w2_codes[:], w2_planes[:], w2_grouped[:].rearrange("p t m j -> p (t m j)"))
+        quantize_z(0, VH)
+        for t in range(PACK):
+            copy_out(t, 0, VH, make_h(t, 0, VH, 0))
+        line_up(3, 1)
+        pool_pairs([(t, 1) for t in range(2, PACK)])
+        quarters = [(VH, VH + VH // 2), (VH + VH // 2, V)]
+        for v0, v1 in quarters:
+            make_z(v0, v1)
+        for v0, v1 in quarters:
+            quantize_z(v0, v1)
+        for t in range(PACK):
+            banks = [make_h(t, v0, v1, 1 - k) for k, (v0, v1) in enumerate(quarters)]
+            for bank, (v0, v1) in zip(banks, quarters):
+                nc.scalar.activation(h_neg_half[t][:, v0:v1], bank[:], ACT.Copy, scale=-0.5)
+            for bank, (v0, v1) in zip(banks, quarters):
+                nc.scalar.copy(h_plain[t][:, v0:v1], bank[:])
 
         out_rows = out.rearrange("(p t) v -> p t v", t=PACK)
         for t in range(PACK):

@@ -22,13 +22,14 @@ BANK = 512
 HALVES = 2
 VH = V // HALVES
 TINY = 1e-30
-W1_VECTOR_M = 40
+RUN = 4
 
 
-def deal_views(grouped, raw, tiles, cols):
-    dst = grouped[:].rearrange("p t m j -> p m j t")[:, cols]
-    src = raw[:].rearrange("p j (m t) -> p m j t", t=PACK)[:, cols, :, tiles]
-    return dst, src
+def deal(nc, grouped, raw, t):
+    nc.scalar.copy(
+        grouped.rearrange("p (a e) j -> p a j e", e=RUN),
+        raw[:].rearrange("p j (a s e d) -> p s d a j e", s=2, e=RUN, d=2)[:, t // 2, t % 2],
+    )
 
 
 def quantize(nc, codes, planes, values):
@@ -64,7 +65,7 @@ def tile_picked_prodpool_none_p_kernel(
         all_scales = keep.tile([P, T], U8, name="all_scales", align_bytes=64)
         w1_raw = keep.tile([P, PACK, H], F32, name="w1_raw", align_bytes=64)
         w2_raw = keep.tile([P, PACK, N], F32, name="w2_raw", align_bytes=64)
-        gain = keep.tile([P, PACK], F32, name="gain")
+        gain = keep.tile([P, 2, 8], F32, name="gain")
 
         nc.sync.dma_start(offs_sb[:], offs)
         for q in range(4):
@@ -77,11 +78,15 @@ def tile_picked_prodpool_none_p_kernel(
             in_=x_words[0].rearrange("p n r -> p (n r)").bitcast(I32),
         )
         nc.sync.dma_start(out=w1_raw[:], in_=w1.rearrange("(p j) c -> p j c", j=PACK))
-        nc.scalar.dma_start(out=gain[:], in_=gn.rearrange("(p t) o -> p (t o)", t=PACK))
+        gain_rows = gn.rearrange("(a s e d) o -> s a e (d o)", s=2, e=RUN, d=2)
+        for s in range(2):
+            nc.scalar.dma_start(out=gain[:, s, 0:2], in_=gain_rows[s])
         nc.sync.dma_start(order_sb[:], order)
-        nc.sync.dma_start(out=w2_raw[:], in_=w2.rearrange("(p j) c -> p j c", j=PACK))
         nc.sync.dma_start(n1_sb[:], n1)
         nc.sync.dma_start(n2_sb[:], n2)
+        w2_rows = w2.rearrange("(a s e d) c -> s a e (d c)", s=2, e=RUN, d=2)
+        for s in range(2):
+            nc.sync.dma_start(out=w2_raw[:, 2 * s : 2 * s + 2, :].rearrange("p d c -> p (d c)"), in_=w2_rows[s])
 
         x_planes = keep.tile([P, S], U8, name="x_planes", align_bytes=64)
         x_codes = keep.tile([P, S], U32, name="x_codes", align_bytes=64)
@@ -91,24 +96,25 @@ def tile_picked_prodpool_none_p_kernel(
         gain_abs = keep.tile([P, PACK], F32, name="gain_abs")
         gain_safe = keep.tile([P, PACK], F32, name="gain_safe")
         gain_inv = keep.tile([P, PACK], F32, name="gain_inv")
-        nc.scalar.activation(gain_abs[:], gain[:], ACT.Abs)
-        nc.vector.scalar_tensor_tensor(gain_safe[:], gain_abs[:], TINY, gain[:], ALU.is_lt, ALU.add)
+        nc.scalar.activation(gain_abs[:].rearrange("p (s d) -> p s d", d=2), gain[:, :, 0:2], ACT.Abs)
+        nc.vector.scalar_tensor_tensor(
+            gain_safe[:].rearrange("p (s d) -> p s d", d=2),
+            gain_abs[:].rearrange("p (s d) -> p s d", d=2),
+            TINY,
+            gain[:, :, 0:2],
+            ALU.is_lt,
+            ALU.add,
+        )
         nc.vector.reciprocal(gain_inv[:], gain_safe[:])
 
-        w1_first = keep.tile([P, 1, P, PACK], BF16, name="w1_first", align_bytes=64)
-        w1_rest = keep.tile([P, PACK - 1, P, PACK], BF16, name="w1_rest", align_bytes=64)
         w1_codes = keep.tile([P, H], U32, name="w1_codes", align_bytes=64)
         w1_planes = keep.tile([P, H], U8, name="w1_planes", align_bytes=64)
-        dst, src = deal_views(w1_first, w1_raw, slice(0, 1), slice(0, P))
-        nc.vector.tensor_copy(dst, src)
-        dst, src = deal_views(w1_rest, w1_raw, slice(1, PACK), slice(0, P))
-        nc.scalar.copy(dst, src)
-
         y = [keep.tile([P, S], F32, name="y%d" % t) for t in range(PACK)]
         for t in range(PACK):
             cols = slice(t * P, (t + 1) * P)
-            grouped = w1_first[:, 0] if t == 0 else w1_rest[:, t - 1]
-            quantize(nc, w1_codes[:, cols], w1_planes[:, cols], grouped.rearrange("p m j -> p (m j)"))
+            grouped = keep.tile([P, P, PACK], BF16, name="w1_grouped%d" % t, align_bytes=64)
+            deal(nc, grouped[:], w1_raw, t)
+            quantize(nc, w1_codes[:, cols], w1_planes[:, cols], grouped[:].rearrange("p m j -> p (m j)"))
             width = BANK // 2 if t == 0 else BANK
             for c in range(S // width):
                 picked = slice(c * width, (c + 1) * width)
@@ -119,12 +125,12 @@ def tile_picked_prodpool_none_p_kernel(
                 else:
                     nc.scalar.activation(y[t][:, picked], bank[:], ACT.Copy, scale=gain_abs[:, t : t + 1])
 
-        w2_grouped = keep.tile([P, PACK, P, PACK], BF16, name="w2_grouped", align_bytes=64)
-        w2_codes = keep.tile([P, N], U32, name="w2_codes", align_bytes=64)
+        w2_grouped = [keep.tile([P, P, PACK], BF16, name="w2_grouped%d" % t, align_bytes=64) for t in range(PACK)]
+        w2_codes = keep.tile([P, P], U32, name="w2_codes", align_bytes=64)
         w2_planes = keep.tile([P, N], U8, name="w2_planes", align_bytes=64)
         h_plain = [keep.tile([P, V], F32, name="h_plain%d" % t) for t in range(PACK)]
         h_neg_half = [keep.tile([P, V], F32, name="h_neg_half%d" % t) for t in range(PACK)]
-        larger = [keep.tile([P, PACK, VH], F32, name="larger%d" % u) for u in range(HALVES)]
+        larger = [keep.tile([P, PACK, VH], F32, name="larger%d" % u, align_bytes=64) for u in range(HALVES)]
         bent = [keep.tile([P, PACK, VH], F32, name="bent%d" % u) for u in range(HALVES)]
         z = keep.tile([P, V, PACK], BF16, name="z", align_bytes=64)
         z_codes = keep.tile([P, V], U32, name="z_codes", align_bytes=64)
@@ -148,41 +154,36 @@ def tile_picked_prodpool_none_p_kernel(
             u = v0 // VH
             inside = slice(v0 - u * VH, v1 - u * VH)
             nc.vector.tensor_tensor(
-                z[:, v0:v1, :].rearrange("p (c i) t -> p c t i", i=2),
-                larger[u][:, :, inside].rearrange("p t (c i) -> p c t i", i=2),
-                bent[u][:, :, inside].rearrange("p t (c i) -> p c t i", i=2),
+                z[:, v0:v1, :].rearrange("p (c i) t -> p c t i", i=4),
+                larger[u][:, :, inside].rearrange("p t (c i) -> p c t i", i=4),
+                bent[u][:, :, inside].rearrange("p t (c i) -> p c t i", i=4),
                 ALU.mult,
             )
 
         def quantize_z(v0, v1):
             quantize(nc, z_codes[:, v0:v1], z_planes[:, v0:v1], z[:, v0:v1, :].rearrange("p v t -> p (v t)"))
 
-        def make_h(t, v0, v1, slot):
-            cols = slice(t * P, (t + 1) * P)
-            bank = psum.tile([P, v1 - v0], F32, name="bank%d" % (2 * t + slot))
-            product(nc, bank[:], w2_codes[:, cols], w2_planes[:, cols], z_codes[:, v0:v1], z_planes[:, v0:v1])
+        def make_h(t, codes, v0, v1, slot):
+            bank = psum.tile([P, v1 - v0], F32, name="bank%d" % slot)
+            product(nc, bank[:], codes, w2_planes[:, t * P : (t + 1) * P], z_codes[:, v0:v1], z_planes[:, v0:v1])
             return bank
-
-        def copy_out(t, v0, v1, bank):
-            nc.scalar.activation(h_neg_half[t][:, v0:v1], bank[:], ACT.Copy, scale=-0.5)
-            nc.scalar.copy(h_plain[t][:, v0:v1], bank[:])
 
         for t in range(2):
             for u in range(HALVES):
                 line_up(t, u)
             pool_pairs([(t, u) for u in range(HALVES)])
-        for m0 in range(0, P, P // 2):
-            dst, src = deal_views(w2_grouped, w2_raw, slice(0, PACK), slice(m0, m0 + P // 2))
-            nc.scalar.copy(dst, src)
+        for t in range(PACK):
+            deal(nc, w2_grouped[t][:], w2_raw, t)
         for t in range(2, PACK):
             line_up(t, 0)
         pool_pairs([(t, 0) for t in range(2, PACK)])
         line_up(2, 1)
         make_z(0, VH)
-        quantize(nc, w2_codes[:], w2_planes[:], w2_grouped[:].rearrange("p t m j -> p (t m j)"))
+        quantize(nc, w2_codes[:], w2_planes[:, 0:P], w2_grouped[0][:].rearrange("p m j -> p (m j)"))
         quantize_z(0, VH)
-        for t in range(PACK):
-            copy_out(t, 0, VH, make_h(t, 0, VH, 0))
+        bank = make_h(0, w2_codes[:], 0, VH, 0)
+        nc.scalar.activation(h_neg_half[0][:, 0:VH], bank[:], ACT.Copy, scale=-0.5)
+        nc.scalar.copy(h_plain[0][:, 0:VH], bank[:])
         line_up(3, 1)
         pool_pairs([(t, 1) for t in range(2, PACK)])
         quarters = [(VH, VH + VH // 2), (VH + VH // 2, V)]
@@ -190,14 +191,20 @@ def tile_picked_prodpool_none_p_kernel(
             make_z(v0, v1)
         for v0, v1 in quarters:
             quantize_z(v0, v1)
-        for t in range(PACK):
-            banks = [make_h(t, v0, v1, 1 - k) for k, (v0, v1) in enumerate(quarters)]
-            for bank, (v0, v1) in zip(banks, quarters):
-                nc.scalar.activation(h_neg_half[t][:, v0:v1], bank[:], ACT.Copy, scale=-0.5)
-            for bank, (v0, v1) in zip(banks, quarters):
-                nc.scalar.copy(h_plain[t][:, v0:v1], bank[:])
+        banks = [make_h(0, w2_codes[:], v0, v1, 1 + k) for k, (v0, v1) in enumerate(quarters)]
+        for bank, (v0, v1) in zip(banks, quarters):
+            nc.scalar.activation(h_neg_half[0][:, v0:v1], bank[:], ACT.Copy, scale=-0.5)
+        for bank, (v0, v1) in zip(banks, quarters):
+            nc.scalar.copy(h_plain[0][:, v0:v1], bank[:])
+        w2_late = keep.tile([P, N - P], U32, name="larger1", align_bytes=64)
+        for t in range(1, PACK):
+            codes = w2_late[:, (t - 1) * P : t * P]
+            quantize(nc, codes, w2_planes[:, t * P : (t + 1) * P], w2_grouped[t][:].rearrange("p m j -> p (m j)"))
+            bank = make_h(t, codes, 0, V, 2 + t)
+            nc.scalar.activation(h_neg_half[t][:], bank[:], ACT.Copy, scale=-0.5)
+            nc.scalar.copy(h_plain[t][:], bank[:])
 
-        out_rows = out.rearrange("(p t) v -> p t v", t=PACK)
+        out_rows = out.rearrange("(a s e d) v -> s d a e v", s=2, e=RUN, d=2)
         for t in range(PACK):
             partial = ring.tile([P, V], F32, name="partial")
             result = keep.tile([P, V], F32, name="result%d" % t)
@@ -207,13 +214,15 @@ def tile_picked_prodpool_none_p_kernel(
                 nc.vector.tensor_tensor(
                     partial[:, places], h_neg_half[t][:].indirect(n1_sb[:, entries]), h_plain[t][:, places], ALU.add
                 )
-            for u in range(HALVES):
-                places = slice(u * VH, (u + 1) * VH)
-                entries = slice(u * VH // LANES, (u + 1) * VH // LANES)
+            pieces = [(0, VH), (VH, V)] if t < PACK - 1 else [(0, VH)] + quarters
+            for v0, v1 in pieces:
                 nc.vector.tensor_tensor(
-                    result[:, places], h_neg_half[t][:].indirect(n2_sb[:, entries]), partial[:, places], ALU.add
+                    result[:, v0:v1],
+                    h_neg_half[t][:].indirect(n2_sb[:, v0 // LANES : v1 // LANES]),
+                    partial[:, v0:v1],
+                    ALU.add,
                 )
                 if t == PACK - 1:
-                    nc.sync.dma_start(out=out_rows[:, t, places], in_=result[:, places])
+                    nc.sync.dma_start(out=out_rows[t // 2, t % 2, :, :, v0:v1], in_=result[:, v0:v1])
             if t < PACK - 1:
-                nc.sync.dma_start(out=out_rows[:, t, :], in_=result[:])
+                nc.sync.dma_start(out=out_rows[t // 2, t % 2], in_=result[:])

@@ -17,23 +17,27 @@ ACT = mybir.ActivationFunctionType
 
 P = 128
 PACK = 4
+RUN = 4
+QUADRANT = 32
 LANES = 16
 BANK = 512
+BANKS = 8
 HALVES = 2
 VH = V // HALVES
+WALK = 4
 TINY = 1e-30
-RUN = 4
+LINE_WORDS = 8
 
 
-def deal(nc, grouped, raw, t):
+def cast_weights(nc, grouped, raw, t):
     nc.scalar.copy(
         grouped.rearrange("p (a e) j -> p a j e", e=RUN),
         raw[:].rearrange("p j (a s e d) -> p s d a j e", s=2, e=RUN, d=2)[:, t // 2, t % 2],
     )
 
 
-def quantize(nc, codes, planes, values):
-    nc.vector.quantize_mx(out=codes.bitcast(FP8X4), scales=planes, in_=values)
+def quantize(nc, codes, planes, grouped):
+    nc.vector.quantize_mx(out=codes.bitcast(FP8X4), scales=planes, in_=grouped.rearrange("p c j -> p (c j)"))
 
 
 def product(nc, bank, w_codes, w_planes, codes, planes):
@@ -46,6 +50,14 @@ def product(nc, bank, w_codes, w_planes, codes, planes):
         start=True,
         stop=True,
     )
+
+
+def by_slot(grouped):
+    return grouped.rearrange("p (c i) t -> p c t i", i=WALK)
+
+
+def by_tile(rows):
+    return rows.rearrange("p t (c i) -> p c t i", i=WALK)
 
 
 def tile_picked_prodpool_none_p_kernel(
@@ -65,13 +77,14 @@ def tile_picked_prodpool_none_p_kernel(
         all_scales = keep.tile([P, T], U8, name="all_scales", align_bytes=64)
         w1_raw = keep.tile([P, PACK, H], F32, name="w1_raw", align_bytes=64)
         w2_raw = keep.tile([P, PACK, N], F32, name="w2_raw", align_bytes=64)
-        gain = keep.tile([P, 2, 8], F32, name="gain")
+        gain = keep.tile([P, 2, LINE_WORDS], F32, name="gain")
 
         nc.sync.dma_start(offs_sb[:], offs)
-        for q in range(4):
+        for q in range(P // QUADRANT):
+            rows = x_scales[0, PACK * q : PACK * (q + 1), :].bitcast(I32)
             nc.sync.dma_start(
-                out=all_scales[32 * q : 32 * q + 32, :].bitcast(I32),
-                in_=x_scales[0, 4 * q : 4 * q + 4, :].bitcast(I32).unsqueeze(0).broadcast_to([8, 4, T // 4]),
+                out=all_scales[QUADRANT * q : QUADRANT * (q + 1), :].bitcast(I32),
+                in_=rows.unsqueeze(0).broadcast_to([QUADRANT // PACK, PACK, T // 4]),
             )
         nc.sync.dma_start(
             out=all_words[:].bitcast(I32),
@@ -97,6 +110,28 @@ def tile_picked_prodpool_none_p_kernel(
         gain_safe = keep.tile([P, PACK], F32, name="gain_safe")
         gain_inv = keep.tile([P, PACK], F32, name="gain_inv")
         nc.scalar.activation(gain_abs[:].rearrange("p (s d) -> p s d", d=2), gain[:, :, 0:2], ACT.Abs)
+
+        w1_codes = keep.tile([P, H], U32, name="w1_codes", align_bytes=64)
+        w1_planes = keep.tile([P, H], U8, name="w1_planes", align_bytes=64)
+        y = [keep.tile([P, S], F32, name="y%d" % t) for t in range(PACK)]
+        for t in range(PACK):
+            cols = slice(t * P, (t + 1) * P)
+            w1_grouped = keep.tile([P, P, PACK], BF16, name="w1_grouped%d" % t, align_bytes=64)
+            cast_weights(nc, w1_grouped[:], w1_raw, t)
+            quantize(nc, w1_codes[:, cols], w1_planes[:, cols], w1_grouped[:])
+
+        for t in range(PACK):
+            cols = slice(t * P, (t + 1) * P)
+            width = BANK // 2 if t == 0 else BANK
+            for c in range(S // width):
+                picked = slice(c * width, (c + 1) * width)
+                bank = psum.tile([P, width], F32, name="bank%d" % (c if t == 0 else (2 * (t + 1) + c) % BANKS))
+                product(nc, bank[:], w1_codes[:, cols], w1_planes[:, cols], x_codes[:, picked], x_planes[:, picked])
+                if t == 0 and c % 2 == 1:
+                    nc.vector.tensor_scalar(y[t][:, picked], bank[:], gain_abs[:, t : t + 1], None, ALU.mult)
+                else:
+                    nc.scalar.activation(y[t][:, picked], bank[:], ACT.Copy, scale=gain_abs[:, t : t + 1])
+
         nc.vector.scalar_tensor_tensor(
             gain_safe[:].rearrange("p (s d) -> p s d", d=2),
             gain_abs[:].rearrange("p (s d) -> p s d", d=2),
@@ -107,34 +142,17 @@ def tile_picked_prodpool_none_p_kernel(
         )
         nc.vector.reciprocal(gain_inv[:], gain_safe[:])
 
-        w1_codes = keep.tile([P, H], U32, name="w1_codes", align_bytes=64)
-        w1_planes = keep.tile([P, H], U8, name="w1_planes", align_bytes=64)
-        y = [keep.tile([P, S], F32, name="y%d" % t) for t in range(PACK)]
-        for t in range(PACK):
-            cols = slice(t * P, (t + 1) * P)
-            grouped = keep.tile([P, P, PACK], BF16, name="w1_grouped%d" % t, align_bytes=64)
-            deal(nc, grouped[:], w1_raw, t)
-            quantize(nc, w1_codes[:, cols], w1_planes[:, cols], grouped[:].rearrange("p m j -> p (m j)"))
-            width = BANK // 2 if t == 0 else BANK
-            for c in range(S // width):
-                picked = slice(c * width, (c + 1) * width)
-                bank = psum.tile([P, width], F32, name="bank%d" % (c if t == 0 else (2 * t + c + 2) % 8))
-                product(nc, bank[:], w1_codes[:, cols], w1_planes[:, cols], x_codes[:, picked], x_planes[:, picked])
-                if t == 0 and c % 2 == 1:
-                    nc.vector.tensor_scalar(y[t][:, picked], bank[:], gain_abs[:, t : t + 1], None, ALU.mult)
-                else:
-                    nc.scalar.activation(y[t][:, picked], bank[:], ACT.Copy, scale=gain_abs[:, t : t + 1])
-
         w2_grouped = [keep.tile([P, P, PACK], BF16, name="w2_grouped%d" % t, align_bytes=64) for t in range(PACK)]
-        w2_codes = keep.tile([P, P], U32, name="w2_codes", align_bytes=64)
+        w2_first_codes = keep.tile([P, P], U32, name="w2_first_codes", align_bytes=64)
         w2_planes = keep.tile([P, N], U8, name="w2_planes", align_bytes=64)
         h_plain = [keep.tile([P, V], F32, name="h_plain%d" % t) for t in range(PACK)]
         h_neg_half = [keep.tile([P, V], F32, name="h_neg_half%d" % t) for t in range(PACK)]
         larger = [keep.tile([P, PACK, VH], F32, name="larger%d" % u, align_bytes=64) for u in range(HALVES)]
-        bent = [keep.tile([P, PACK, VH], F32, name="bent%d" % u) for u in range(HALVES)]
+        tanh_smaller = [keep.tile([P, PACK, VH], F32, name="tanh_smaller%d" % u) for u in range(HALVES)]
         z = keep.tile([P, V, PACK], BF16, name="z", align_bytes=64)
         z_codes = keep.tile([P, V], U32, name="z_codes", align_bytes=64)
         z_planes = keep.tile([P, V], U8, name="z_planes", align_bytes=64)
+        z_rows = keep.tile([P, PACK, VH], BF16, name="z_rows", align_bytes=64)
         lined = {}
 
         def line_up(t, u):
@@ -142,70 +160,68 @@ def tile_picked_prodpool_none_p_kernel(
             entries = slice(u * 2 * VH // LANES, (u + 1) * 2 * VH // LANES)
             nc.vector.tensor_copy(lined[t, u][:], y[t][:].indirect(order_sb[:, entries]))
 
-        def pool_pairs(jobs):
-            for t, u in jobs:
-                smaller = keep.tile([P, VH], F32, name="smaller%d_%d" % (t, u))
-                nc.vector.tensor_tensor(smaller[:], lined[t, u][:, 0::2], lined[t, u][:, 1::2], ALU.min)
-                nc.scalar.activation(bent[u][:, t, :], smaller[:], ACT.Tanh, scale=gain_inv[:, t : t + 1])
+        def pool_pairs(jobs, tag):
+            smaller = keep.tile([P, len(jobs), VH], F32, name=tag, align_bytes=64)
+            for k, (t, u) in enumerate(jobs):
+                nc.vector.tensor_tensor(smaller[:, k, :], lined[t, u][:, 0::2], lined[t, u][:, 1::2], ALU.min)
+                nc.scalar.activation(tanh_smaller[u][:, t, :], smaller[:, k, :], ACT.Tanh, scale=gain_inv[:, t : t + 1])
             for t, u in jobs:
                 nc.vector.tensor_tensor(larger[u][:, t, :], lined[t, u][:, 0::2], lined[t, u][:, 1::2], ALU.max)
+                if u == 0:
+                    nc.gpsimd.tensor_tensor(z_rows[:, t, :], larger[u][:, t, :], tanh_smaller[u][:, t, :], ALU.mult)
 
-        def make_z(v0, v1):
-            u = v0 // VH
-            inside = slice(v0 - u * VH, v1 - u * VH)
-            nc.vector.tensor_tensor(
-                z[:, v0:v1, :].rearrange("p (c i) t -> p c t i", i=4),
-                larger[u][:, :, inside].rearrange("p t (c i) -> p c t i", i=4),
-                bent[u][:, :, inside].rearrange("p t (c i) -> p c t i", i=4),
-                ALU.mult,
-            )
-
-        def quantize_z(v0, v1):
-            quantize(nc, z_codes[:, v0:v1], z_planes[:, v0:v1], z[:, v0:v1, :].rearrange("p v t -> p (v t)"))
-
-        def make_h(t, codes, v0, v1, slot):
-            bank = psum.tile([P, v1 - v0], F32, name="bank%d" % slot)
-            product(nc, bank[:], codes, w2_planes[:, t * P : (t + 1) * P], z_codes[:, v0:v1], z_planes[:, v0:v1])
+        def make_h(t, w_codes, v0, v1, bank_number):
+            bank = psum.tile([P, v1 - v0], F32, name="bank%d" % bank_number)
+            product(nc, bank[:], w_codes, w2_planes[:, t * P : (t + 1) * P], z_codes[:, v0:v1], z_planes[:, v0:v1])
             return bank
 
         for t in range(2):
             for u in range(HALVES):
                 line_up(t, u)
-            pool_pairs([(t, u) for u in range(HALVES)])
+            pool_pairs([(t, u) for u in range(HALVES)], "smaller%d" % t)
         for t in range(PACK):
-            deal(nc, w2_grouped[t][:], w2_raw, t)
+            cast_weights(nc, w2_grouped[t][:], w2_raw, t)
+        quantize(nc, w2_first_codes[:], w2_planes[:, 0:P], w2_grouped[0][:])
         for t in range(2, PACK):
             line_up(t, 0)
-        pool_pairs([(t, 0) for t in range(2, PACK)])
-        line_up(2, 1)
-        make_z(0, VH)
-        quantize(nc, w2_codes[:], w2_planes[:, 0:P], w2_grouped[0][:].rearrange("p m j -> p (m j)"))
-        quantize_z(0, VH)
-        bank = make_h(0, w2_codes[:], 0, VH, 0)
+        pool_pairs([(t, 0) for t in range(2, PACK)], "smaller2")
+        nc.scalar.copy(by_slot(z[:, 0:VH, :]), by_tile(z_rows[:]))
+        for t in range(2, PACK):
+            line_up(t, 1)
+        pool_pairs([(t, 1) for t in range(2, PACK)], "z_rows")
+        quantize(nc, z_codes[:, 0:VH], z_planes[:, 0:VH], z[:, 0:VH, :])
+        bank = make_h(0, w2_first_codes[:], 0, VH, 0)
         nc.scalar.activation(h_neg_half[0][:, 0:VH], bank[:], ACT.Copy, scale=-0.5)
         nc.scalar.copy(h_plain[0][:, 0:VH], bank[:])
-        line_up(3, 1)
-        pool_pairs([(t, 1) for t in range(2, PACK)])
+
         quarters = [(VH, VH + VH // 2), (VH + VH // 2, V)]
         for v0, v1 in quarters:
-            make_z(v0, v1)
+            inside = slice(v0 - VH, v1 - VH)
+            nc.vector.tensor_tensor(
+                by_slot(z[:, v0:v1, :]),
+                by_tile(larger[1][:, :, inside]),
+                by_tile(tanh_smaller[1][:, :, inside]),
+                ALU.mult,
+            )
         for v0, v1 in quarters:
-            quantize_z(v0, v1)
-        banks = [make_h(0, w2_codes[:], v0, v1, 1 + k) for k, (v0, v1) in enumerate(quarters)]
+            quantize(nc, z_codes[:, v0:v1], z_planes[:, v0:v1], z[:, v0:v1, :])
+        banks = [make_h(0, w2_first_codes[:], v0, v1, 1 + k) for k, (v0, v1) in enumerate(quarters)]
         for bank, (v0, v1) in zip(banks, quarters):
             nc.scalar.activation(h_neg_half[0][:, v0:v1], bank[:], ACT.Copy, scale=-0.5)
         for bank, (v0, v1) in zip(banks, quarters):
             nc.scalar.copy(h_plain[0][:, v0:v1], bank[:])
-        w2_late = keep.tile([P, N - P], U32, name="larger1", align_bytes=64)
+
+        w2_late_codes = keep.tile([P, N - P], U32, name="larger1", align_bytes=64)
         for t in range(1, PACK):
-            codes = w2_late[:, (t - 1) * P : t * P]
-            quantize(nc, codes, w2_planes[:, t * P : (t + 1) * P], w2_grouped[t][:].rearrange("p m j -> p (m j)"))
-            bank = make_h(t, codes, 0, V, 2 + t)
+            w_codes = w2_late_codes[:, (t - 1) * P : t * P]
+            quantize(nc, w_codes, w2_planes[:, t * P : (t + 1) * P], w2_grouped[t][:])
+            bank = make_h(t, w_codes, 0, V, len(quarters) + t)
             nc.scalar.activation(h_neg_half[t][:], bank[:], ACT.Copy, scale=-0.5)
             nc.scalar.copy(h_plain[t][:], bank[:])
 
         out_rows = out.rearrange("(a s e d) v -> s d a e v", s=2, e=RUN, d=2)
         for t in range(PACK):
+            last = t == PACK - 1
             partial = ring.tile([P, V], F32, name="partial")
             result = keep.tile([P, V], F32, name="result%d" % t)
             for u in range(HALVES):
@@ -214,15 +230,14 @@ def tile_picked_prodpool_none_p_kernel(
                 nc.vector.tensor_tensor(
                     partial[:, places], h_neg_half[t][:].indirect(n1_sb[:, entries]), h_plain[t][:, places], ALU.add
                 )
-            pieces = [(0, VH), (VH, V)] if t < PACK - 1 else [(0, VH)] + quarters
-            for v0, v1 in pieces:
+            for v0, v1 in ([(0, VH)] + quarters if last else [(0, VH), (VH, V)]):
                 nc.vector.tensor_tensor(
                     result[:, v0:v1],
                     h_neg_half[t][:].indirect(n2_sb[:, v0 // LANES : v1 // LANES]),
                     partial[:, v0:v1],
                     ALU.add,
                 )
-                if t == PACK - 1:
+                if last:
                     nc.sync.dma_start(out=out_rows[t // 2, t % 2, :, :, v0:v1], in_=result[:, v0:v1])
-            if t < PACK - 1:
+            if not last:
                 nc.sync.dma_start(out=out_rows[t // 2, t % 2], in_=result[:])

from contextlib import ExitStack

import concourse.mybir as mybir

K, T, S, V, N, H = 512, 2048, 1024, 512, 512, 512
FLOPS = 2 * K * H * S + 2 * H * N * V

F32 = mybir.dt.float32
BF16 = mybir.dt.bfloat16
I32 = mybir.dt.int32
U32 = mybir.dt.uint32
U16 = mybir.dt.uint16
U8 = mybir.dt.uint8
FP8X4 = mybir.dt.float8_e4m3fn_x4
ALU = mybir.AluOpType
ACT = mybir.ActivationFunctionType

P = 128
PACK = 4
RUN = 4
QUADRANT = 32
LANES = 16
BANK = 512
BANKS = 8
HALVES = 2
VH = V // HALVES
WALK = 4
TINY = 1e-30
LINE_WORDS = 8


def cast_weights(nc, grouped, raw, t):
    nc.scalar.copy(
        grouped.rearrange("p (a e) j -> p a j e", e=RUN),
        raw[:].rearrange("p j (a s e d) -> p s d a j e", s=2, e=RUN, d=2)[:, t // 2, t % 2],
    )


def quantize(nc, codes, planes, grouped):
    nc.vector.quantize_mx(out=codes.bitcast(FP8X4), scales=planes, in_=grouped.rearrange("p c j -> p (c j)"))


def product(nc, bank, w_codes, w_planes, codes, planes):
    nc.tensor.matmul_mx(
        out=bank,
        lhsT=w_codes.bitcast(FP8X4),
        lhsT_scale=w_planes,
        rhs=codes.bitcast(FP8X4),
        rhs_scale=planes,
        start=True,
        stop=True,
    )


def by_slot(grouped):
    return grouped.rearrange("p (c i) t -> p c t i", i=WALK)


def by_tile(rows):
    return rows.rearrange("p t (c i) -> p c t i", i=WALK)


def tile_picked_prodpool_none_p_kernel(
    tc, x_words, x_scales, w1, gn, w2, offs, order, n1, n2, out
):
    nc = tc.nc
    with ExitStack() as ctx:
        keep = ctx.enter_context(tc.tile_pool(name="keep", bufs=1))
        ring = ctx.enter_context(tc.tile_pool(name="ring", bufs=3))
        psum = ctx.enter_context(tc.psum_pool(name="psum", bufs=1))

        offs_sb = keep.tile([P, S // LANES], U16, name="offs_sb")
        order_sb = keep.tile([P, S // LANES], U16, name="order_sb")
        n1_sb = keep.tile([P, V // LANES], U16, name="n1_sb")
        n2_sb = keep.tile([P, V // LANES], U16, name="n2_sb")
        all_words = keep.tile([P, T], U32, name="all_words", align_bytes=64)
        all_scales = keep.tile([P, T], U8, name="all_scales", align_bytes=64)
        w1_raw = keep.tile([P, PACK, H], F32, name="w1_raw", align_bytes=64)
        w2_raw = keep.tile([P, PACK, N], F32, name="w2_raw", align_bytes=64)
        gain = keep.tile([P, 2, LINE_WORDS], F32, name="gain")

        nc.sync.dma_start(offs_sb[:], offs)
        for q in range(P // QUADRANT):
            rows = x_scales[0, PACK * q : PACK * (q + 1), :].bitcast(I32)
            nc.sync.dma_start(
                out=all_scales[QUADRANT * q : QUADRANT * (q + 1), :].bitcast(I32),
                in_=rows.unsqueeze(0).broadcast_to([QUADRANT // PACK, PACK, T // 4]),
            )
        nc.sync.dma_start(
            out=all_words[:].bitcast(I32),
            in_=x_words[0].rearrange("p n r -> p (n r)").bitcast(I32),
        )
        nc.sync.dma_start(out=w1_raw[:], in_=w1.rearrange("(p j) c -> p j c", j=PACK))
        gain_rows = gn.rearrange("(a s e d) o -> s a e (d o)", s=2, e=RUN, d=2)
        for s in range(2):
            nc.scalar.dma_start(out=gain[:, s, 0:2], in_=gain_rows[s])
        nc.sync.dma_start(order_sb[:], order)
        nc.sync.dma_start(n1_sb[:], n1)
        nc.sync.dma_start(n2_sb[:], n2)
        w2_rows = w2.rearrange("(a s e d) c -> s a e (d c)", s=2, e=RUN, d=2)
        for s in range(2):
            nc.sync.dma_start(out=w2_raw[:, 2 * s : 2 * s + 2, :].rearrange("p d c -> p (d c)"), in_=w2_rows[s])

        x_planes = keep.tile([P, S], U8, name="x_planes", align_bytes=64)
        x_codes = keep.tile([P, S], U32, name="x_codes", align_bytes=64)
        nc.vector.tensor_copy(x_planes[:], all_scales[:].indirect(offs_sb[:]))
        nc.vector.tensor_copy(x_codes[:], all_words[:].indirect(offs_sb[:]))

        gain_abs = keep.tile([P, PACK], F32, name="gain_abs")
        gain_safe = keep.tile([P, PACK], F32, name="gain_safe")
        gain_inv = keep.tile([P, PACK], F32, name="gain_inv")
        nc.scalar.activation(gain_abs[:].rearrange("p (s d) -> p s d", d=2), gain[:, :, 0:2], ACT.Abs)

        w1_codes = keep.tile([P, H], U32, name="w1_codes", align_bytes=64)
        w1_planes = keep.tile([P, H], U8, name="w1_planes", align_bytes=64)
        y = [keep.tile([P, S], F32, name="y%d" % t) for t in range(PACK)]
        for t in range(PACK):
            cols = slice(t * P, (t + 1) * P)
            w1_grouped = keep.tile([P, P, PACK], BF16, name="w1_grouped%d" % t, align_bytes=64)
            cast_weights(nc, w1_grouped[:], w1_raw, t)
            quantize(nc, w1_codes[:, cols], w1_planes[:, cols], w1_grouped[:])

        for t in range(PACK):
            cols = slice(t * P, (t + 1) * P)
            width = BANK // 2 if t == 0 else BANK
            for c in range(S // width):
                picked = slice(c * width, (c + 1) * width)
                bank = psum.tile([P, width], F32, name="bank%d" % (c if t == 0 else (2 * (t + 1) + c) % BANKS))
                product(nc, bank[:], w1_codes[:, cols], w1_planes[:, cols], x_codes[:, picked], x_planes[:, picked])
                if t == 0 and c % 2 == 1:
                    nc.vector.tensor_scalar(y[t][:, picked], bank[:], gain_abs[:, t : t + 1], None, ALU.mult)
                else:
                    nc.scalar.activation(y[t][:, picked], bank[:], ACT.Copy, scale=gain_abs[:, t : t + 1])

        nc.vector.scalar_tensor_tensor(
            gain_safe[:].rearrange("p (s d) -> p s d", d=2),
            gain_abs[:].rearrange("p (s d) -> p s d", d=2),
            TINY,
            gain[:, :, 0:2],
            ALU.is_lt,
            ALU.add,
        )
        nc.vector.reciprocal(gain_inv[:], gain_safe[:])

        w2_grouped = [keep.tile([P, P, PACK], BF16, name="w2_grouped%d" % t, align_bytes=64) for t in range(PACK)]
        w2_first_codes = keep.tile([P, P], U32, name="w2_first_codes", align_bytes=64)
        w2_planes = keep.tile([P, N], U8, name="w2_planes", align_bytes=64)
        h_plain = [keep.tile([P, V], F32, name="h_plain%d" % t) for t in range(PACK)]
        h_neg_half = [keep.tile([P, V], F32, name="h_neg_half%d" % t) for t in range(PACK)]
        larger = [keep.tile([P, PACK, VH], F32, name="larger%d" % u, align_bytes=64) for u in range(HALVES)]
        tanh_smaller = [keep.tile([P, PACK, VH], F32, name="tanh_smaller%d" % u) for u in range(HALVES)]
        z = keep.tile([P, V, PACK], BF16, name="z", align_bytes=64)
        z_codes = keep.tile([P, V], U32, name="z_codes", align_bytes=64)
        z_planes = keep.tile([P, V], U8, name="z_planes", align_bytes=64)
        z_rows = keep.tile([P, PACK, VH], BF16, name="z_rows", align_bytes=64)
        lined = {}

        def line_up(t, u):
            lined[t, u] = keep.tile([P, 2 * VH], F32, name="lined%d_%d" % (t, u))
            entries = slice(u * 2 * VH // LANES, (u + 1) * 2 * VH // LANES)
            nc.vector.tensor_copy(lined[t, u][:], y[t][:].indirect(order_sb[:, entries]))

        def pool_pairs(jobs, tag):
            smaller = keep.tile([P, len(jobs), VH], F32, name=tag, align_bytes=64)
            for k, (t, u) in enumerate(jobs):
                nc.vector.tensor_tensor(smaller[:, k, :], lined[t, u][:, 0::2], lined[t, u][:, 1::2], ALU.min)
                nc.scalar.activation(tanh_smaller[u][:, t, :], smaller[:, k, :], ACT.Tanh, scale=gain_inv[:, t : t + 1])
            for t, u in jobs:
                nc.vector.tensor_tensor(larger[u][:, t, :], lined[t, u][:, 0::2], lined[t, u][:, 1::2], ALU.max)
                if u == 0:
                    nc.gpsimd.tensor_tensor(z_rows[:, t, :], larger[u][:, t, :], tanh_smaller[u][:, t, :], ALU.mult)

        def make_h(t, w_codes, v0, v1, bank_number):
            bank = psum.tile([P, v1 - v0], F32, name="bank%d" % bank_number)
            product(nc, bank[:], w_codes, w2_planes[:, t * P : (t + 1) * P], z_codes[:, v0:v1], z_planes[:, v0:v1])
            return bank

        for t in range(2):
            for u in range(HALVES):
                line_up(t, u)
            pool_pairs([(t, u) for u in range(HALVES)], "smaller%d" % t)
        for t in range(PACK):
            cast_weights(nc, w2_grouped[t][:], w2_raw, t)
        quantize(nc, w2_first_codes[:], w2_planes[:, 0:P], w2_grouped[0][:])
        for t in range(2, PACK):
            line_up(t, 0)
        pool_pairs([(t, 0) for t in range(2, PACK)], "smaller2")
        nc.scalar.copy(by_slot(z[:, 0:VH, :]), by_tile(z_rows[:]))
        for t in range(2, PACK):
            line_up(t, 1)
        pool_pairs([(t, 1) for t in range(2, PACK)], "z_rows")
        quantize(nc, z_codes[:, 0:VH], z_planes[:, 0:VH], z[:, 0:VH, :])
        bank = make_h(0, w2_first_codes[:], 0, VH, 0)
        nc.scalar.activation(h_neg_half[0][:, 0:VH], bank[:], ACT.Copy, scale=-0.5)
        nc.scalar.copy(h_plain[0][:, 0:VH], bank[:])

        quarters = [(VH, VH + VH // 2), (VH + VH // 2, V)]
        for v0, v1 in quarters:
            inside = slice(v0 - VH, v1 - VH)
            nc.vector.tensor_tensor(
                by_slot(z[:, v0:v1, :]),
                by_tile(larger[1][:, :, inside]),
                by_tile(tanh_smaller[1][:, :, inside]),
                ALU.mult,
            )
        for v0, v1 in quarters:
            quantize(nc, z_codes[:, v0:v1], z_planes[:, v0:v1], z[:, v0:v1, :])
        banks = [make_h(0, w2_first_codes[:], v0, v1, 1 + k) for k, (v0, v1) in enumerate(quarters)]
        for bank, (v0, v1) in zip(banks, quarters):
            nc.scalar.activation(h_neg_half[0][:, v0:v1], bank[:], ACT.Copy, scale=-0.5)
        for bank, (v0, v1) in zip(banks, quarters):
            nc.scalar.copy(h_plain[0][:, v0:v1], bank[:])

        w2_late_codes = keep.tile([P, N - P], U32, name="larger1", align_bytes=64)
        for t in range(1, PACK):
            w_codes = w2_late_codes[:, (t - 1) * P : t * P]
            quantize(nc, w_codes, w2_planes[:, t * P : (t + 1) * P], w2_grouped[t][:])
            bank = make_h(t, w_codes, 0, V, len(quarters) + t)
            nc.scalar.activation(h_neg_half[t][:], bank[:], ACT.Copy, scale=-0.5)
            nc.scalar.copy(h_plain[t][:], bank[:])

        out_rows = out.rearrange("(a s e d) v -> s d a e v", s=2, e=RUN, d=2)
        for t in range(PACK):
            last = t == PACK - 1
            partial = ring.tile([P, V], F32, name="partial")
            result = keep.tile([P, V], F32, name="result%d" % t)
            for u in range(HALVES):
                places = slice(u * VH, (u + 1) * VH)
                entries = slice(u * VH // LANES, (u + 1) * VH // LANES)
                nc.vector.tensor_tensor(
                    partial[:, places], h_neg_half[t][:].indirect(n1_sb[:, entries]), h_plain[t][:, places], ALU.add
                )
            for v0, v1 in ([(0, VH)] + quarters if last else [(0, VH), (VH, V)]):
                nc.vector.tensor_tensor(
                    result[:, v0:v1],
                    h_neg_half[t][:].indirect(n2_sb[:, v0 // LANES : v1 // LANES]),
                    partial[:, v0:v1],
                    ALU.add,
                )
                if last:
                    nc.sync.dma_start(out=out_rows[t // 2, t % 2, :, :, v0:v1], in_=result[:, v0:v1])
            if not last:
                nc.sync.dma_start(out=out_rows[t // 2, t % 2], in_=result[:])
